import numpy as np, ml_dtypes
CORES = [2,42,66,74,82,90,114]
N = 7
import mx_ref
NC, G = 128, 4
C = np.float32(0.0133)
FROM = [[5,3,4,1,0,6,2],[2,3,6,0,5,4,1],[2,4,1,6,0,3,5]]
BF = ml_dtypes.bfloat16
def cut(t, i, w=512):
    return t[:, w * i:w * i + w]
def tile(rs):
    return np.stack(rs, axis=2).reshape(128, -1).astype(BF)
def layer(w, X):
    out = []
    for i in range(G):
        for t in range(len(X)):
            p = mx_ref.matmul(mx_ref.quantize(cut(w, len(X) * i + t)), X[t])
            z = p if t == 0 else z + p
        out.append(z)
    return out
def act(Z):
    return [np.maximum(z, 0) * C for z in Z]
def setup_inputs(rng):
    def f(*shape):
        return mx_ref.flush((rng.standard_normal(shape, dtype=np.float32) * np.exp2(rng.integers(-2, 3, shape[:-1] + (1,)))).astype(BF))
    return {"x": f(N, 128, 4 * NC), "w": f(N, 128, 2 * 2 * G * 512), "v": f(N, 128, 2 * 512)}
def setup_inputs_blocks(rng):
    d = setup_inputs(rng)
    for k in ("x", "v"): d[k] = mx_ref.spread(d[k], rng, 4)
    for k in ("w",): d[k] = mx_ref.spread(d[k], rng, 2)
    return d
def setup_inputs_wide(rng):
    d = setup_inputs(rng)
    for k in ("x", "w", "v"): d[k] = mx_ref.flush((d[k].astype(np.float32) * np.exp2(rng.integers(-5, 6, (N, 1, 1))).astype(np.float32)).astype(BF))
    return d
def reference(x, w, v):
    a = [mx_ref.quantize(x[r]) for r in range(N)]
    for l in range(2):
        a = [mx_ref.quantize(tile(act(layer(cut(w[r], l, 2 * G * 512), [a[r], a[FROM[l][r]]])))) for r in range(N)]
    y = np.zeros((N, 128, NC), np.float32)
    for r in range(N):
        y[r] = mx_ref.matmul(mx_ref.quantize(cut(v[r], 0)), a[r]) + mx_ref.matmul(mx_ref.quantize(cut(v[r], 1)), a[FROM[2][r]])
    return {"y": y}

from concourse.mybir import dt, AluOpType, ActivationFunctionType

NC = 128
TW = 4 * NC
G = 4
NL = 2
WT = 2 * G
C = 0.0133
BANK = 512

SCRATCH = {
    "xb": ("sbuf", [128, TW], "bfloat16"),
    "wb": ("sbuf", [128, NL * WT * TW], "bfloat16"),
    "vb": ("sbuf", [128, 2 * TW], "bfloat16"),
    "wq": ("sbuf", [128, NL * WT * NC], "float8_e4m3fn_x4"),
    "wp": ("sbuf", [128, NL * WT * NC], "uint8"),
    "vq": ("sbuf", [128, 2 * NC], "float8_e4m3fn_x4"),
    "vp": ("sbuf", [128, 2 * NC], "uint8"),
    "h1": ("sbuf", [128, TW], "bfloat16"),
    "h2": ("sbuf", [128, TW], "bfloat16"),
    "yb": ("sbuf", [128, NC], "float32"),
    "ps": ("psum", [128, NL * G * BANK], "float32"),
}
for _l in range(NL + 1):
    SCRATCH["aq%d" % _l] = ("sbuf", [128, NC], "float8_e4m3fn_x4")
    SCRATCH["ap%d" % _l] = ("sbuf", [128, NC], "uint8")
    SCRATCH["rq%d" % _l] = ("sbuf", [128, NC], "float8_e4m3fn_x4")
    SCRATCH["rp%d" % _l] = ("sbuf", [128, NC], "uint8")

SEMAPHORES = (["ldx", "ldv", "qv", "mmy", "ycp", "yd"]
              + ["ld%d" % l for l in range(NL)]
              + ["qw%d%d" % (l, h) for l in range(NL) for h in range(2)]
              + ["mm%d%d" % (l, i) for l in range(NL) for i in range(G)]
              + ["act%d" % l for l in range(NL)]
              + ["qa%d" % l for l in range(NL + 1)]
              + ["arr%d" % l for l in range(NL + 1)]
              + ["sent%d" % l for l in range(NL + 1)])


def _masks(topo, src, dst, l):
    full = topo.mask(src, dst)
    if l > 0:
        return full, full
    eng = [b for b in range(full.bit_length()) if (full >> b) & 1]
    return sum(1 << b for b in eng[0::2]), sum(1 << b for b in eng[1::2])


def _count(masks):
    return sum(bin(m).count("1") for m in masks)


def rank_program(g, core, T, topo):
    rank = T.rank_of(core)
    if rank is None:
        return
    FROM = T.tables["FROM"]
    cores = T.cores
    S = T.sem
    ten, vec, sca, syn = g.tensor, g.vector, g.scalar, g.sync
    half = WT * TW

    dsts = [[cores[q] for q in range(len(cores)) if FROM[l][q] == rank] for l in range(NL + 1)]
    n_sent = [sum(_count(_masks(topo, core, d, l)) for d in dsts[l]) for l in range(NL + 1)]
    n_arr = [_count(_masks(topo, cores[FROM[l][rank]], core, l)) for l in range(NL + 1)]

    def bank(b):
        return T.ps[:, BANK * b:BANK * b + NC]

    def wtile(l, i, t):
        k = WT * l + 2 * i + t
        return T.wq[:, NC * k:NC * (k + 1)], T.wp[:, NC * k:NC * (k + 1)]

    syn.dma_start(T.xb[:], T.x[:]).then_inc(S.ldx, 16)
    syn.dma_start(T.wb[:, 0:half], T.w[:, 0:half]).then_inc(S.ld0, 16)
    syn.wait_ge(S.sent0, n_sent[0])
    syn.dma_start(T.wb[:, half:2 * half], T.w[:, half:2 * half]).then_inc(S.ld1, 16)
    syn.wait_ge(S.sent1, n_sent[1])
    syn.dma_start(T.vb[:], T.v[:]).then_inc(S.ldv, 16)
    syn.wait_ge(S.ycp, 1)
    syn.dma_start(T.y[:], T.yb[:]).then_inc(S.yd, 16)
    syn.wait_ge(S.yd, 16)

    for l in range(NL + 1):
        g.wait_ge(S["qa%d" % l], 1)
        for d in dsts[l]:
            if not topo.may_write(core, d):
                raise ValueError("no direct write from core %d to core %d" % (core, d))
            rid, pid, _se = topo.addr(d)
            m_codes, m_plane = _masks(topo, core, d, l)
            g.remote_dma(T["rq%d" % l][:].bitcast(dt.uint8), T["aq%d" % l][:].bitcast(dt.uint8),
                         S["arr%d" % l], S["sent%d" % l], pid, rid, m_codes)
            g.remote_dma(T["rp%d" % l][:], T["ap%d" % l][:],
                         S["arr%d" % l], S["sent%d" % l], pid, rid, m_plane)
    for l in range(NL + 1):
        g.wait_ge(S["sent%d" % l], n_sent[l])

    vec.wait_ge(S.ldx, 16)
    vec.quantize_mx(T.aq0[:], T.ap0[:], T.xb[:]).then_inc(S.qa0, 1)
    for l in range(NL):
        vec.wait_ge(S["ld%d" % l], 16)
        for h in range(2):
            c0 = (2 * l + h) * 4
            vec.quantize_mx(T.wq[:, NC * c0:NC * (c0 + 4)], T.wp[:, NC * c0:NC * (c0 + 4)],
                            T.wb[:, TW * c0:TW * (c0 + 4)]).then_inc(S["qw%d%d" % (l, h)], 1)
        tile = T["h%d" % (l + 1)]
        for i in range(1, G, 2):
            vec.wait_ge(S["mm%d%d" % (l, i)], 1)
            vec.tensor_scalar(tile[:, i:TW:G], bank(G * l + i), 0.0, C,
                              AluOpType.max, AluOpType.mult).then_inc(S["act%d" % l], 1)
        vec.wait_ge(S["act%d" % l], G)
        vec.quantize_mx(T["aq%d" % (l + 1)][:], T["ap%d" % (l + 1)][:], tile[:]).then_inc(S["qa%d" % (l + 1)], 1)
    vec.wait_ge(S.ldv, 16)
    vec.quantize_mx(T.vq[:], T.vp[:], T.vb[:]).then_inc(S.qv, 1)
    vec.wait_ge(S.mmy, 1)
    vec.tensor_copy(T.yb[:], bank(0)).then_inc(S.ycp, 1)

    for l in range(NL):
        tile = T["h%d" % (l + 1)]
        for i in range(0, G, 2):
            sca.wait_ge(S["mm%d%d" % (l, i)], 1)
            sca.activation(tile[:, i:TW:G], bank(G * l + i), ActivationFunctionType.Relu,
                           scale=C).then_inc(S["act%d" % l], 1)

    for l in range(NL):
        ten.wait_ge(S["qa%d" % l], 1)
        for i in range(G):
            if i % 2 == 0:
                ten.wait_ge(S["qw%d%d" % (l, i // 2)], 1)
            wc, ws = wtile(l, i, 0)
            ten.matmul_mx(bank(G * l + i), wc, ws, T["aq%d" % l][:], T["ap%d" % l][:], True, False)
        ten.wait_ge(S["arr%d" % l], n_arr[l])
        for i in range(G):
            wc, ws = wtile(l, i, 1)
            ten.matmul_mx(bank(G * l + i), wc, ws, T["rq%d" % l][:], T["rp%d" % l][:],
                          False, True).then_inc(S["mm%d%d" % (l, i)], 1)
    ten.wait_ge(S["qa%d" % NL], 1)
    ten.wait_ge(S.qv, 1)
    ten.matmul_mx(bank(0), T.vq[:, 0:NC], T.vp[:, 0:NC], T["aq%d" % NL][:], T["ap%d" % NL][:], True, False)
    ten.wait_ge(S["arr%d" % NL], n_arr[NL])
    ten.matmul_mx(bank(0), T.vq[:, NC:2 * NC], T.vp[:, NC:2 * NC], T["rq%d" % NL][:], T["rp%d" % NL][:],
                  False, True).then_inc(S.mmy, 1)
